import numpy as np, ml_dtypes
CORES = [5,29,101,125,133,157,229,253]
N = 8
BF = ml_dtypes.bfloat16
def gentries(a):
    return np.ascontiguousarray(a.reshape(8, 16, -1).transpose(0, 2, 1)).reshape(8, -1)
def gtable(e):
    e = np.asarray(e); return np.ascontiguousarray(e.reshape(8, -1, 16).transpose(0, 2, 1)).reshape(128, -1).astype(np.int32)
C, F, P, CAP, L, T, RO = 1536, 2048, 256, 16, 2, 3, 4
def parts(rng):
    return dict(su=rng.integers(0, F, (N, 8, 16, C)), se=rng.integers(0, 2, (N, 8, 16, C)), pw=rng.integers(-7, 8, (N, 8, 16, F)), ot=rng.integers(0, C, (N, 8, L, F)),
                x=rng.integers(0, 16, (N, 8, 16, P)), dr=rng.integers(0, 16, (N, 8, 16, P)), c=rng.integers(0, C, (N, 8, P)),
                th=rng.choice(np.array([8, 9, 10, 10, 11, 11, 12, 17]), (N, 8, P)), hw=rng.integers(-7, 8, (N, 8, 16, 2)))
def pack(s):
    def b(a): return np.ascontiguousarray(a.reshape(N, 128, -1)).astype(np.float32).astype(BF)
    return {"sf": np.ascontiguousarray((2 * s["su"] + s["se"]).reshape(N, 128, C)).astype(np.int32), "pw": b(s["pw"]), "ot": np.ascontiguousarray(s["ot"].reshape(N, 8 * L, F)).astype(np.int32),
            "x0": b(s["x"]), "dr": b(s["dr"]), "c0": np.stack([gtable(a) for a in s["c"]]), "th": np.stack([gtable(a) for a in s["th"]]), "hw": b(s["hw"])}
def setup_inputs(rng):
    return pack(parts(rng))
def behind(rng, s, g):
    n = 2 * CAP; q = C // 4; e = np.arange(C)
    s["pw"][:, g] = rng.integers(1, 8, (N, 16, F)); s["x"][:, g] = rng.integers(1, 16, (N, 16, P))
    half = np.argsort(rng.random((N, 16, C)), axis=1) % 2
    s["se"][:, g] = np.where(e < q, 0, np.where(e < 2 * q, half, np.where(e < C - n, 1, 0)))
    s["ot"][:, g] = rng.integers(2 * q, C - n, (N, L, F)); s["c"][:, g] = rng.integers(0, q, (N, P)); s["th"][:, g] = rng.integers(0, 17, (N, P))
    o = np.stack([rng.permutation(P) for r in range(N)]); ask, late = o[:, :n], o[:, n:2 * n]
    for k in range(N):
        r = (k - 1) % N; y = s["x"][r, g][:, ask[r]]
        u = np.add.reduce(s["hw"][k, g][:, :, None] * y[:, None, :], axis=0); h = ((u[0] * u[1]) >> 5) & (F - 1)
        s["pw"][k, g][:, h] = np.array([1, -2] + [0] * 14)[:, None]
        s["ot"][k, g, 0, h] = rng.integers(q, 2 * q, n); s["ot"][k, g, 1, h] = rng.integers(0, q, n)
        free = np.setdiff1d(np.arange(F), h); mine = free[free % N == (k + 1) % N]
        s["su"][k, g] = rng.choice(free, (16, C)); b = rng.permutation(np.arange(2 * q, C - n))[:n]
        s["su"][k, g][:, b] = rng.choice(mine, (16, n))
        s["su"][k, g][:, C - n:] = h[rng.integers(0, n, (16, n))]; s["su"][k, g, 0, C - n:] = h
        s["c"][k, g, ask[k]] = b; s["th"][k, g, ask[k]] = rng.integers(1, 9, n)
        s["c"][k, g, late[k]] = C - n + np.arange(n); s["th"][k, g, late[k]] = rng.integers(9, 17, n)
    for k in range(N):
        s["x"][k, g, 0, late[k]] = 2 * T - 3; s["x"][k, g, 1, late[k]] = 0; s["dr"][k, g, 0, late[k]] = 0; s["dr"][k, g, 1, late[k]] = 1
def setup_inputs_room(rng):
    s = parts(rng); s["su"] = s["su"] - s["su"] % N + np.arange(C) % N
    for r in range(N):
        for g in range(0, 8, 2):
            n = rng.choice(np.array([0, 1, CAP - 1, CAP, CAP + 1, 2 * CAP]), N)
            if g == 0: n[(r + 1) % N] = CAP
            if g == 2: n[(r + 1) % N] = CAP + 1
            if g == 4: n[(r + 2) % N] = 2 * CAP
            k = np.full(P, -1); w = np.repeat(np.arange(N), n); k[:len(w)] = w; k = rng.permutation(k)
            s["c"][r, g] = rng.integers(0, C // N, P) * N + np.where(k < 0, rng.integers(0, N, P), k)
            s["th"][r, g] = np.where(k < 0, 0, 17)
    s["th"][:, 1] = 0
    s["th"][:, 3] = 17; s["pw"][:, 3] = rng.integers(1, 8, (N, 16, F)); s["se"][:, 3] = 0; s["x"][:, 3] = rng.integers(1, 16, (N, 16, P))
    for r in range(0, N, 2): s["c"][r, 3] = rng.integers(0, C // N, P) * N + (r + 1) % N
    s["pw"][:, 5] = rng.integers(5, 8, (N, 16, F)); s["se"][:, 5] = 1; s["x"][:, 5] = rng.integers(13, 16, (N, 16, P))
    s["th"][:, 5] = np.where(s["c"][:, 5] % N == N - 1, 0, rng.integers(1, 18, (N, P)))
    for p, e, k in ((0, 0, 0), (P - 1, C - 1, F - 1)):
        s["c"][:, 5, p] = e; s["th"][:, 5, p] = 17; s["su"][:, 5, :, e] = k
    behind(rng, s, 7)
    return pack(s)
def setup_inputs_ties(rng):
    s = parts(rng); five = rng.integers(0, F, (N, 8, 5, C))
    s["su"] = np.take_along_axis(five, rng.integers(0, 5, (N, 8, 16, C)), 2)
    s["pw"] = rng.integers(-1, 2, s["pw"].shape) * (rng.random(s["pw"].shape) < 0.4)
    s["x"] = rng.integers(0, 2, s["x"].shape); s["dr"] = rng.choice(np.array([0, 0, 1, 15]), s["dr"].shape)
    s["th"] = rng.integers(8, 18, (N, 8, P))
    for p, t in ((3, 17), (5, 16), (P - 1, 17)): s["x"][..., p] = 0; s["dr"][..., p] = 0; s["th"][..., p] = t
    return pack(s)
def turn(rng, s, g):
    h = C // 2
    s["pw"][:, g] = rng.integers(1, 8, (N, 16, F)); s["se"][:, g] = np.where(np.arange(C) < h, 1, 0)
    s["x"][:, g] = rng.integers(1, 16, (N, 16, P)); s["th"][:, g] = rng.integers(1, 17, (N, P))
    s["ot"][:, g, 0] = rng.integers(0, h, (N, F)); s["ot"][:, g, 1] = rng.integers(h, C, (N, F))
def setup_inputs_alike(rng):
    s = parts(rng); pool = rng.integers(0, F, (N, 8, 1, 12)); pool[..., 0] = 0; pool[..., 1] = F - 1
    s["su"] = np.take_along_axis(pool, rng.integers(0, 12, (N, 8, 16 * C))[:, :, None, :], 3).reshape(N, 8, 16, C)
    t = rng.integers(0, 8, P)
    for k in ("x", "dr", "c"): s[k][:, ::2] = s[k][:, ::2][..., t]
    h = C // 2; turn(rng, s, 1); turn(rng, s, 3)
    for r in range(N):
        k = np.full(P, 1); k[1 + rng.permutation(P - 2)[:int(rng.integers(65, 125))]] = 0; k[0] = 0; k[P - 1] = 2
        s["su"][r, 1, :, :h] = np.array([0, int(rng.integers(1, F - 1)), F - 1])[np.arange(h) % 3]
        s["c"][r, 1] = k + 3 * rng.integers(0, h // 3, P)
        o = rng.permutation(F)[:F // P * P].reshape(P, F // P); e = rng.permutation(h)[:P]
        s["su"][r, 3][:, e] = o[np.arange(P)[None, :], rng.integers(0, F // P, (16, P))]
        s["c"][r, 3] = e
    return pack(s)
def setup_inputs_ends(rng):
    s = parts(rng)
    s["su"] = np.where(rng.random(s["su"].shape) < 0.3, rng.choice(np.array([0, F - 1]), s["su"].shape), s["su"])
    s["ot"] = np.where(rng.random(s["ot"].shape) < 0.4, rng.choice(np.array([0, C - 1]), s["ot"].shape), s["ot"])
    s["c"] = np.where(rng.random(s["c"].shape) < 0.4, rng.choice(np.array([0, C - 1]), s["c"].shape), s["c"])
    s["pw"] = rng.choice(np.array([-7, 7]), s["pw"].shape)
    s["x"] = rng.choice(np.array([0, 15]), s["x"].shape); s["dr"] = rng.choice(np.array([0, 1, 15]), s["dr"].shape)
    s["th"] = rng.choice(np.array([0, 1, 8, 9, 10, 11, 16, 17]), s["th"].shape)
    s["hw"] = rng.choice(np.array([-7, 7]), s["hw"].shape); s["hw"][:, 0] = 7; s["hw"][:, 1, :, 0] = 7; s["hw"][:, 1, :, 1] = -7
    for p in (0, 7, P - 1): s["x"][..., p] = 15; s["dr"][..., p] = 0; s["th"][..., p] = 17
    return pack(s)
def setup_inputs_spread(rng):
    s = parts(rng)
    s["pw"] = np.rint(s["pw"] * rng.random((N, 8, 1, F))).astype(np.int64)
    s["x"] = (16 * rng.random((N, 8, 1, P)) * rng.random((N, 8, 16, P))).astype(np.int64)
    s["dr"] = (16 * rng.random((N, 8, 1, P)) * rng.random((N, 8, 16, P))).astype(np.int64)
    s["su"] = np.minimum((F * rng.random((N, 8, 16, C)) ** 3).astype(np.int64), F - 1)
    s["ot"] = np.minimum((C * rng.random((N, 8, L, F)) ** 2).astype(np.int64), C - 1)
    s["c"] = np.minimum((C * rng.random((N, 8, P)) ** 4).astype(np.int64), C - 1)
    s["th"] = rng.integers(0, 18, (N, 8, P))
    return pack(s)
def check_inputs(d):
    bad = []
    for k, lo, hi in (("sf", 0, 2 * F - 1), ("pw", -7, 7), ("ot", 0, C - 1), ("x0", 0, 15), ("dr", 0, 15), ("c0", 0, C - 1), ("th", 0, 17), ("hw", -7, 7)):
        a = np.asarray(d[k]).astype(np.float64)
        if not np.all((a >= lo) & (a <= hi) & (a == np.rint(a))): bad.append("range of " + k)
    return bad
def lowest(m, f):
    lane = np.broadcast_to(np.arange(P), m.shape); key = np.arange(N * 8).reshape(N, 8, 1) * F + f
    first = np.full(N * 8 * F, P); np.minimum.at(first, key[m], lane[m])
    return m & (first[key] == lane)
def reference(sf, pw, ot, x0, dr, c0, th, hw):
    cells = sf.astype(np.int64).reshape(N, 8, 16, C); w = pw.astype(np.float32).astype(np.int32).reshape(N, 8, 16, F); o = ot.astype(np.int64).reshape(N, 8, L, F)
    x = x0.astype(np.float32).astype(np.int32).reshape(N, 8, 16, P); step = dr.astype(np.float32).astype(np.int32).reshape(N, 8, 16, P); hv = hw.astype(np.float32).astype(np.int64).reshape(N, 8, 16, 2)
    c = np.stack([gentries(a) for a in c0]).astype(np.int64); t = np.stack([gentries(a) for a in th]).astype(np.int64)
    d = c.copy(); j = np.full((N, 8, P), -1); f = np.zeros((N, 8, P), np.int64)
    rk = np.arange(N)[:, None, None]; gr = np.arange(8)[None, :, None]
    for rnd in range(RO):
        for sub in range(T):
            live = j < L
            code = np.take_along_axis(cells, d[:, :, None, :], 3); su = code >> 1
            v = np.stack([np.add.reduce(np.take_along_axis(w, su[:, :, i:i + 1], 3) * x, axis=2) for i in range(16)], axis=2)
            v = np.where((code & 1) == 1, -v, v)
            inside = live & (np.add.reduce((v >= 0).astype(np.int64), axis=2) >= t); miss = live & ~inside
            a, b, p = np.nonzero(lowest(inside & (j > 0), f)); ff, jj = f[a, b, p], j[a, b, p]
            up, lo = o[a, b, jj - 1, ff], o[a, b, jj, ff]
            o[a, b, jj - 1, ff] = lo; o[a, b, jj, ff] = up
            c = np.where(inside, d, c); x = np.where(inside[:, :, None, :], (x + step) & 15, x)
            least = np.take_along_axis(su, np.argmin(v, axis=2)[:, :, None, :], 2)[:, :, 0]
            f = np.where(miss & (j == -1), least, f)
            j = np.where(inside, -1, np.where(miss, j + 1, j))
            d = np.where(miss & (j < L), o[rk, gr, np.clip(j, 0, L - 1), f], d)
        wait = j == L; q = f % N; served = np.zeros((N, 8, P), bool)
        for k in range(N):
            m = wait & (q == k); n = m.astype(np.int64)
            served = served | (m & (np.add.accumulate(n, axis=2) - n < CAP))
        wq = hv[q, gr]; xt = x.transpose(0, 1, 3, 2).astype(np.int64)
        h = ((np.add.reduce(xt * wq[..., 0], axis=3) * np.add.reduce(xt * wq[..., 1], axis=3)) >> 5) & (F - 1)
        ans = o[q, gr, 0, h]
        a, b, p = np.nonzero(lowest(served, f)); o[a, b, L - 1, f[a, b, p]] = ans[a, b, p]
        d = np.where(served, ans, d); j = np.where(served, L - 1, j)
    return {"yt": o.reshape(N, 8 * L, F).astype(np.float32), "yc": np.stack([gtable(a) for a in c]).astype(np.float32), "yx": x.reshape(N, 128, P).astype(np.float32)}

import math
from concourse.bass import DstId, RemoteDMATransfer
from concourse.mybir import AluOpType as OP, ActivationFunctionType as AF

NSUB, PER = 12, 3
F32, BF, F16, I32, U16 = "float32", "bfloat16", "float16", "int32", "uint16"
WIDE = {
    I32: dict(sfi=1536, sf2i=1536, oi=256),
    F32: dict(sf2=1536, stl=256, mh=128, df=128, mn=512, pcol=8, mk=8, qc=128, cb=64, ag=1280, tw=224, so=256, yxs=256, yts=256),
    BF: dict(pwl=2048, pw2=4096, xa=13 * 256, drs=256, xc=256, xsg=256, wg=4096, zz=4112, oht=256, lb=2048, rb=2048, ge=512, cs=512,
             mb=32, io1=144, io2=128, iog=128, ir=192, t1=144, pt=144, idp=128, idn=128, idk=128, id8=128, bo=128, tge=128, id2=32,
             oh32=32, rs0=192, rsb=192, hwt=16, rh=2, wq=128, wsc=128, ohf=256, sm2=256, uw=512),
    F16: dict(sm=256, om=256, rd=2048, z=16 * 13, pr=16 * 9, cst=16, om2=256, dk=16),
    U16: dict(cod=256, sbuf16=4 * 128, rl=4 * 128, agu=4 * 1024, q16=32, fx16=32),
}
PACK = {
    "kf": (F32, "thv miss ycs yy w100 e300 fhk lk ib key kk k2 sv sv_ wk0 wk wk2 wr wr5 old us w2 dl0 dl"),
    "ki": (I32, "c0i thi mi mi_ mj mj_ gi ga gb f2i fhi fli pi pmi q2i hp hl hh c16 q128 ha hb"),
    "ku": (U16, "xo16 d16 m16 oh16 oo16 bc16 fl16"),
}
SCRATCH = {n: ("sbuf", [128, w], d) for d, t in WIDE.items() for n, w in t.items()}
SCRATCH.update({n: ("sbuf", [128, 16 * len(s.split())], d) for n, (d, s) in PACK.items()})
SCRATCH.update({n: ("psum", [128, 512], F32) for n in ("pv0", "pv1", "pg", "pdd", "pc", "ps", "pf", "px")})
PLACE = {v: (n, 16 * i) for n, (d, s) in PACK.items() for i, v in enumerate(s.split())}
LOADS = ["l_c0", "l_sf", "l_th", "l_ot0", "l_ot1", "l_pw", "l_pw2", "l_x0", "l_dr", "l_hw", "o_c", "o_x", "o_t0", "o_t1"]
SEMAPHORES = (["e_v", "e_s", "e_t", "e_g", "sent", "hwa", "hwr"] + LOADS
              + ["ad%d" % r for r in range(4)] + ["ar%d" % r for r in range(4)] + ["rr%d" % r for r in range(4)])
CHUNKS = [("pv0", 0, 6), ("pv1", 6, 12), ("ps", 12, 16)]
PA = [("s", 0, 3), ("v", 3, 6), ("s", 6, 9), ("v", 9, 12), ("s", 12, 14), ("c", 0), ("v", 14, 15), ("s", 15, 16), ("c", 1), ("c", 2)]
PB = [("s", 0, 4), ("v", 4, 6), ("e",), ("s", 6, 9), ("v", 9, 12), ("s", 12, 14), ("c", 0), ("s", 14, 16), ("c", 1), ("c", 2)]
PC = [("s", 0, 4), ("v", 4, 6), ("e",), ("s", 6, 10), ("v", 10, 12), ("s", 12, 14), ("c", 0), ("s", 14, 16), ("c", 1), ("c", 2)]
RELAYS = 4


def routes(T, topo):
    out = []
    for c in T.cores:
        others = [d for d in T.cores if d != c]
        direct = [d for d in others if topo.may_write(c, d)]
        cross = [d for d in others if not topo.may_write(c, d)]
        cand = [h for h in topo.cores_of(c) if T.rank_of(h) is None and all(topo.may_write(h, d) for d in cross)]
        k = min(RELAYS, len(cross), len(cand))
        out.append((direct, [(cand[i], cross[i::k]) for i in range(k)]))
    return out


def split_engines(eng, k):
    n = 1
    while 2 * n * k <= len(eng):
        n *= 2
    return [sum(1 << e for e in eng[i * n:(i + 1) * n]) for i in range(k)], n


def dst(topo, d, src):
    rid, pid = topo.addr(d, src)
    return DstId(rid=rid, pnc=pid)


def relay_program(g, core, T, topo, owner, dests):
    masks, n = split_engines(topo.engines(core, dests[0]), len(dests))
    first = split_engines(topo.engines(T.cores[owner], core), len(routes(T, topo)[owner][1]))[1]
    msgs = [("hwr", T.rh[:, 0:2], T.hwt[:, 2 * owner:2 * owner + 2], "hwa")]
    for r in range(4):
        o = r * 1024 + owner * 128
        msgs.append(("rr%d" % r, T.rl[:, r * 128:(r + 1) * 128], T.agu[:, o:o + 128], "ar%d" % r))
    for sem, src, land, arr in msgs:
        g.wait_ge(T.sem[sem], first)
        g.remote_dma_fused([RemoteDMATransfer(dst_ids=[dst(topo, d, core)], dma_engine_mask=m, remote_sem=T.sem[arr],
                                              src=src, dst=land) for d, m in zip(dests, masks)], local_sem=T.sem.sent)
    g.wait_ge(T.sem.sent, n * len(dests) * len(msgs))


def rank_program(g, core, T, topo):
    rank = T.rank_of(core)
    rt = routes(T, topo)
    if rank is None:
        for owner in range(len(rt)):
            for h, dests in rt[owner][1]:
                if h == core:
                    relay_program(g, core, T, topo, owner, dests)
        return
    Q = {"v": g.vector, "s": g.scalar, "t": g.tensor, "g": g, "y": g.sync}
    ops = []
    acc = {}

    def A(name, lo=0, hi=None, step=1, part=None):
        if name in PLACE:
            hi = 16 if hi is None else hi
            name, o = PLACE[name]
            lo, hi = lo + o, hi + o
        if hi is None:
            hi = SCRATCH[name][1][1]
        if SCRATCH[name][0] == "psum":
            m = 1
        elif step == 1:
            m = ((1 << (hi - lo)) - 1) << lo
        else:
            m = sum(1 << i for i in range(lo, hi, step))
        if part is not None:
            return (T[name][part:part + 16, lo:hi], [(name, m)])
        return (T[name][:, lo:hi:step] if step != 1 else T[name][:, lo:hi], [(name, m)])

    def IND(win, off):
        return (win[0].indirect(off[0]), win[1] + off[1])

    def rec(q, call, rd, wr, sem=None, cnt=0):
        me = len(ops)
        deps = set()
        for name, m in rd:
            w, r = acc.setdefault(name, ([], {}))
            deps.update(o for k, o in w if k & m)
            if SCRATCH[name][0] == "psum":
                deps.update(o for (qq, k), o in r.items() if qq != q)
        for name, m in wr:
            w, r = acc.setdefault(name, ([], {}))
            deps.update(o for k, o in w if k & m)
            deps.update(o for (qq, k), o in r.items() if k & m)
        for name, m in rd:
            acc[name][1][(q if sem is None else me, m)] = me
        for name, m in wr:
            w, r = acc[name]
            nw = [[k & ~m, o] for k, o in w if k & ~m] + [[m, me]]
            nr = {}
            for (qq, k), o in r.items():
                if k & ~m:
                    nr[(qq, k & ~m)] = max(o, nr.get((qq, k & ~m), -1))
            acc[name] = (nw, nr)
        deps.discard(me)
        if q == "t":
            deps = {o for o in deps if ops[o][0] != "t"}
        ops.append([q, call, deps, sem, cnt])

    def regs(*xs):
        return [r for x in xs if isinstance(x, tuple) for r in x[1]]

    def val(x):
        return x[0] if isinstance(x, tuple) else x

    def tt(out, a, b, op):
        rec("v", lambda: g.vector.tensor_tensor(out[0], a[0], b[0], op), regs(a, b), out[1])

    def ts(out, a, s1, op0, s2=None, op1=None):
        if op1 is None:
            rec("v", lambda: g.vector.tensor_scalar(out[0], a[0], val(s1), None, op0), regs(a, s1), out[1])
        else:
            rec("v", lambda: g.vector.tensor_scalar(out[0], a[0], val(s1), val(s2), op0, op1), regs(a, s1, s2), out[1])

    def cp(out, a):
        rec("v", lambda: g.vector.tensor_copy(out[0], a[0]), a[1], out[1])

    def ms(out, c):
        rec("v", lambda: g.vector.memset(out[0], c), [], out[1])

    def scan(out, d0, d1, op0, op1):
        rec("v", lambda: g.vector.tensor_tensor_scan(out[0], d0[0], d1[0], 0.0, op0, op1), regs(d0, d1), out[1])

    def act(out, a, func, bias=None, scale=None):
        kw = {}
        if bias is not None:
            kw["bias"] = val(bias)
        if scale is not None:
            kw["scale"] = val(scale)
        rec("s", lambda: g.scalar.activation(out[0], a[0], func, **kw), regs(a, bias, scale), out[1])

    def mm(out, l, r, start, stop):
        rec("t", lambda: g.tensor.matmul(out[0], l[0], r[0], start, stop), regs(l, r), out[1])

    def iota(out, pat, base, cm, small=True):
        if small:
            rec("g", lambda: g.iota(out[0], pat, base, cm, allow_small_or_imprecise_dtypes=True), [], out[1])
        else:
            rec("g", lambda: g.iota(out[0], pat, base, cm), [], out[1])

    def dma(q, out, a, sem):
        rec(q, lambda: Q[q].dma_start(val(out), val(a)), regs(a), regs(out), sem, 16)

    def arrive(wr, sem, cnt):
        rec("x", None, [], wr, sem, cnt)

    def to_list(out, src, n, first):
        for a in range(16):
            mm(out, A("t1", 15 - a, 143 - a), A(src, a, 16 * n, 16), first and a == 0, a == 15)

    def zs(i, n=1):
        return A("z", 16 * i, 16 * (i + n))

    def prs(i, n=1):
        return A("pr", 16 * i, 16 * (i + n))

    def col(name, b):
        return A(name, b, b + 1)

    row0, row1 = A("ag", 0, 256, 2), A("ag", 1, 256, 2)
    direct, relays = rt[rank]
    nsent = [0]

    def send(src, land, rland, sem_d, sem_r):
        masks, n = split_engines(topo.engines(core, relays[0][0]), len(relays))
        tr = [RemoteDMATransfer(dst_ids=[dst(topo, h, core)], dma_engine_mask=m, remote_sem=T.sem[sem_r], src=src[0], dst=rland)
              for (h, ds), m in zip(relays, masks)]
        rec("g", lambda: g.remote_dma_fused(tr, local_sem=T.sem.sent), src[1], [], "sent", -1)
        md, nd = split_engines(topo.engines(core, direct[0]), 1)
        tr2 = [RemoteDMATransfer(dst_ids=[dst(topo, d, core) for d in direct], dma_engine_mask=md[0], remote_sem=T.sem[sem_d],
                                 srcs=[src[0]], dsts=[land] * len(direct))]
        rec("g", lambda: g.remote_dma_fused(tr2, local_sem=T.sem.sent), src[1], [], "sent", -1)
        nsent[0] += n * len(relays) + nd

    from_direct = [q for q in range(len(rt)) if core in rt[q][0]]
    from_relay = [q for q in range(len(rt)) if q != rank and q not in from_direct]
    n_direct = sum(split_engines(topo.engines(T.cores[q], core), 1)[1] for q in from_direct)
    n_relay = sum(split_engines(topo.engines(h, ds[0]), len(ds))[1] for q in from_relay for h, ds in rt[q][1] if core in ds)

    dma("y", A("sfi"), T.sf[:], "l_sf")
    dma("y", A("pwl", 0, 1024), T.pw[:, 0:1024], "l_pw")
    dma("y", A("pwl", 1024, 2048), T.pw[:, 1024:2048], "l_pw2")
    dma("s", A("hwt", 2 * rank, 2 * rank + 2), T.hw[:], "l_hw")
    dma("s", A("xa", 0, 256), T.x0[:], "l_x0")
    dma("s", A("c0i"), T.c0[:], "l_c0")
    dma("y", A("thi"), T.th[:], "l_th")
    dma("y", A("drs"), T.dr[:], "l_dr")
    dma("y", A("oi", 0, 128), T.ot[0:16:2, :], "l_ot0")
    dma("y", A("oi", 128, 256), T.ot[1:16:2, :], "l_ot1")
    iota(A("pi"), [[0, 16]], 0, 1, False)
    iota(A("iog"), [[16, 8], [0, 16]], 0, 0)
    iota(A("io1"), [[1, 144]], 0, 0)
    iota(A("ir"), [[0, 12], [1, 16]], 0, 0)
    iota(A("ib"), [[16, 16]], 0, 0)
    iota(A("io2"), [[2, 128]], 0, 0)
    iota(A("qc"), [[1, 8], [0, 16]], -100, 0)
    send(A("hwt", 2 * rank, 2 * rank + 2), T.hwt[:, 2 * rank:2 * rank + 2], T.rh[:, 0:2], "hwa", "hwr")
    arrive([r for q in range(len(rt)) if q != rank for r in A("hwt", 2 * q, 2 * q + 2)[1]], "hwa", n_direct + n_relay)

    def zrep(src, g0, g1):
        for k in range(g0, g1):
            act(A("zz", 8 + k, 8 + 4096, 16), A(src, 0, 256), AF.Copy, scale=col("mk", k))

    ms(A("zz"), 0.0)
    ts(A("pmi"), A("pi"), 15, OP.bitwise_and)
    ms(A("rs0"), 1.0)
    ms(A("rsb"), 0.0)
    tt(col("pcol", 1), col("pi", 0), col("pmi", 0), OP.subtract)
    ms(A("cb"), 0.0)
    ms(A("so"), 0.0)
    ts(A("mk"), A("iog", 0, 128, 16), col("pcol", 1), OP.is_equal, 32.0, OP.mult)
    zrep("xa", 0, 8)
    ms(A("rs0", 0, 192, 16), 0.0)
    ms(A("rsb", 0, 192, 16), 1.0e6)
    ms(A("cb", 0, 16), 1.0)
    ms(A("cb", 48, 64), 1.0)
    ms(A("c16"), 16)
    cp(col("pcol", 0), col("pi", 0))
    cp(col("pcol", 2), col("pmi", 0))
    cp(A("bc16"), A("pmi"))
    ts(col("pcol", 3), col("pcol", 1), 15.0, OP.add)
    ts(col("pcol", 4), col("pcol", 2), 2.0, OP.mult, 1.0, OP.add)
    ts(col("pcol", 5), col("pcol", 2), 16.0, OP.add)
    ts(A("yy"), A("ib"), col("pcol", 2), OP.add, -1.0 / 256, OP.mult)
    ts(A("idp"), A("io1", 0, 128), col("pcol", 0), OP.is_equal)
    ts(col("ga", 0), col("pi", 0), 7, OP.bitwise_and)
    ts(col("ga", 1), col("pi", 0), 3, OP.arith_shift_right, 12, OP.bitwise_and)
    ts(col("ga", 2), col("pi", 0), 3, OP.arith_shift_right, 1, OP.bitwise_and)
    ts(col("ga", 3), col("pi", 0), 16, OP.bitwise_and)
    ts(col("gb", 0), col("ga", 0), 16.0, OP.mult, 2.0, OP.add)
    tt(col("gb", 1), col("ga", 1), col("ga", 2), OP.add)
    ts(col("gb", 2), col("ga", 3), 100.0, OP.mult)
    tt(col("gb", 3), col("gb", 0), col("gb", 1), OP.add)
    ts(A("t1"), A("io1"), col("pcol", 3), OP.is_equal)
    tt(col("pcol", 6), col("gb", 3), col("gb", 2), OP.add)
    ts(A("idn"), A("io1", 0, 128), col("pcol", 0), OP.is_equal, -1.0, OP.mult)
    ts(A("pt"), A("io1"), col("pcol", 6), OP.is_equal)
    ts(A("idk"), A("io1", 0, 128), col("pcol", 0), OP.is_equal, 4096.0, OP.mult)
    ts(A("id8"), A("io1", 0, 128), col("pcol", 0), OP.is_equal, -8.0, OP.mult)
    ts(A("id2"), A("io1", 0, 32), col("pcol", 4), OP.is_equal)
    ts(A("oh32"), A("io1", 0, 32), col("pcol", 5), OP.is_equal)
    ts(A("bo"), A("iog"), col("pcol", 1), OP.is_equal)
    ts(A("tge"), A("io1", 0, 128), col("pcol", 0), OP.is_le, -1.0, OP.mult)
    cp(A("d16"), A("c0i"))
    tt(A("tge"), A("tge"), A("bo"), OP.mult)
    cp(zs(11), A("c0i"))
    cp(A("cst"), A("c0i"))
    ts(zs(12), A("c0i"), 0.0, OP.mult)
    ts(prs(5, 4), A("cb"), 0.0, OP.mult)

    def pre_j():
        tt(zs(0, 4), prs(5, 4), A("cb"), OP.is_le)
        ts(zs(7, 4), prs(5, 4), 1.0, OP.add, 3.0, OP.min)

    def pre_d():
        tt(zs(4, 2), zs(0, 2), zs(11, 2), OP.mult)
        tt(zs(6), A("cst"), zs(11), OP.subtract)

    pre_j()
    pre_d()
    cp(A("cod"), IND(A("sfi"), A("d16")))
    ts(A("sf2i"), A("sfi"), 4094, OP.bitwise_and)
    act(A("pw2", 1, 2048, 2), A("pwl", 0, 1024), AF.Copy, scale=-1.0)
    cp(A("pw2", 0, 2048, 2), A("pwl", 0, 1024))
    cp(A("pw2", 2048, 4096, 2), A("pwl", 1024, 2048))
    ts(A("pw2", 2049, 4096, 2), A("pwl", 1024, 2048), -1.0, OP.mult)
    cp(A("thv"), A("thi"))

    def lists_init():
        cp(row0, A("oi", 0, 128))
        cp(row1, A("oi", 128, 256))
        tt(A("df"), A("oi", 0, 128), A("oi", 128, 256), OP.add)
        ts(A("mh"), A("df"), 0.5, OP.mult)
        tt(A("df"), A("oi", 128, 256), A("mh"), OP.subtract)

    def build_l():
        ts(A("fli"), A("gi"), 8, OP.arith_shift_right, 15, OP.bitwise_and)
        ts(A("lk"), A("fli"), col("pcol", 1), OP.add)
        for b in range(16):
            ts(A("lb", 128 * b, 128 * b + 128), A("io1", 0, 128), col("lk", b), OP.is_equal)

    def folds(buf, sc, op1, b0, b1):
        for b in range(b0, b1):
            ts(A(buf, 128 * b, 128 * b + 128), A("io2"), col("fhk", b), OP.is_equal, col(sc, b), op1)
            mm(A("pc", 0, 128), A("lb", 128 * b, 128 * b + 128), A(buf, 128 * b, 128 * b + 128), b == 0, b == 15)

    def writers(part):
        if part == 0:
            tt(A("sm2"), IND(A("so"), A("fx16", 0, 16)), A("ohf"), OP.mult)
            to_list(A("pf", 0, 16), "sm2", 16, True)
            return
        ts(A("wk2"), A("wk"), 2.0, OP.mult)
        cp(A("old"), A("pg", 16, 32))
        tt(A("wr"), A("pf", 0, 16), A("wk2"), OP.is_lt)
        ts(A("wr5"), A("wr"), 0.5, OP.mult)

    def write_row1():
        tt(A("dl0"), zs(11), A("old"), OP.subtract)
        tt(A("dl"), A("dl0"), A("wr5"), OP.mult)
        folds("rd", "dl", OP.mult, 0, 16)

    def write_row1_end():
        tt(A("df"), A("df"), A("pc", 0, 128), OP.add)
        tt(A("mh"), A("mh"), A("pc", 0, 128), OP.add)

    def next_x(t, part):
        xp = A("xa", 256 * (t - 1), 256 * t)
        if part == 0:
            mm(A("px", 0, 256), A("idp"), xp, True, False)
            mm(A("px", 0, 256), A("idp"), A("drs"), False, True)
        elif part == 1:
            act(A("xsg"), A("px", 0, 256), AF.Sign, bias=-15.5)
        else:
            mm(A("px", 256, 512), A("idp"), xp, True, False)
            mm(A("px", 256, 512), A("idp"), A("drs"), False, False)
            mm(A("px", 256, 512), A("id8"), A("xsg"), False, True)
            act(A("xa", 256 * t, 256 * (t + 1)), A("px", 256, 512), AF.Identity, bias=-8.0)

    def swap():
        act(A("ps", 0, 128), A("pc", 0, 128), AF.Sign, bias=0.5, scale=-1.0)

    def swap_end(r):
        tt(A("pf", 0, 128), A("df"), A("ps", 0, 128), OP.mult)
        tt(row0, A("mh"), A("pf", 0, 128), OP.subtract)
        if r is not None:
            sb = A("sbuf16", 128 * r, 128 * r + 128)
            cp(sb, row0)
            o = r * 1024 + rank * 128
            send(sb, T.agu[:, o:o + 128], T.rl[:, 128 * r:128 * r + 128], "ad%d" % r, "rr%d" % r)
        tt(row1, A("mh"), A("pf", 0, 128), OP.add)

    G = A("pg", 0, 16)
    D = A("pdd", 0, 16)

    def new_d():
        cp(A("d16"), D)
        cp(A("cod", 0, 64), IND(A("sfi"), A("d16", 0, 4)))
        cp(A("cod", 64, 256), IND(A("sfi"), A("d16", 4, 16)))
        cp(zs(11), D)
        pre_d()

    for t in range(1, NSUB + 1):
        last = t == NSUB
        exch = t % PER == 0
        reorder = t >= 3
        after_exch = t > 1 and (t - 1) % PER == 0
        r = t // PER - 1
        opened = set()
        for step in (PC if t == 1 or after_exch else PB if t % 2 else PA):
            if step[0] == "e":
                if t == 1:
                    cp(A("sf2"), A("sf2i"))
                if after_exch:
                    writers(1)
                    write_row1()
                if t % 2 and t not in (1, 7):
                    build_l()
                continue
            if step[0] == "c":
                bank, b0, b1 = CHUNKS[step[1]]
                lo, hi, src = 32 * b0, 32 * b1, A(bank, 0, 32 * (b1 - b0))
                if step[1] == 0:
                    next_x(t, 0)
                if step[1] == 2:
                    next_x(t, 1)
                    if not last:
                        act(A("stl"), IND(A("sf2"), A("d16")), AF.Copy)
                ts(A("ge", lo, hi), src, 0.0, OP.is_ge)
                if not last:
                    scan(A("mn", lo, hi), A("rsb", 0, hi - lo), src, OP.add, OP.min)
                scan(A("cs", lo, hi), A("rs0", 0, hi - lo), A("ge", lo, hi), OP.mult, OP.add)
                if step[1] == 1 and after_exch:
                    write_row1_end()
                continue
            e, g0, g1 = step
            wout, win = A("wg", 256 * g0, 256 * g1), IND(A("pw2"), A("cod", 16 * g0, 16 * g1))
            if e == "v":
                cp(wout, win)
            else:
                act(wout, win, AF.Copy)
            bank, b0, b1 = [c for c in CHUNKS if c[1] <= g0 < c[2]][0]
            whole, half_i = A(bank, 0, 32 * (b1 - b0)), A("ir", 0, 32 * (b1 - b0))
            if bank not in opened:
                opened.add(bank)
                mm(whole, A("idp"), half_i, True, False)
            for p in range(16 * g0, 16 * g1):
                b, a = p // 16, p % 16
                o = 32 * (b - b0) + 16 * (a // 2 % 2)
                z0 = 8 + 16 * p - 8 * (a % 2)
                mm(A(bank, o, o + 16, part=32 * (a // 4)), A("zz", z0, z0 + 16), A("wg", 16 * p, 16 * p + 16), False, False)
            if g1 == b1:
                mm(whole, A("idp"), half_i, False, True)
        for h in range(2):
            mm(G, A("pt", 2 - 2 * h, 130 - 2 * h), A("cs", 15 + 16 * h, 512, 32), h == 0, h == 1)
        next_x(t, 2)
        if not last:
            cp(A("mi", 0, 32), A("mn", 15, 512, 16))
        tt(A("miss"), G, A("thv"), OP.is_lt)
        if not last:
            ts(A("mj", 0, 32), A("mi", 0, 32), 31, OP.bitwise_and)
        if exch:
            folds("rb", "miss", OP.is_gt, 0, 16)
            swap()
        tt(A("yy"), A("yy"), A("miss"), OP.add)
        if not last:
            cp(A("mb"), A("mj", 0, 32))
        tt(A("pr"), IND(A("miss"), A("bc16", 0, 9)), zs(2, 9), OP.mult)
        ts(A("xo16"), A("yy"), -256.0, OP.mult, 256.0 * t, OP.add)
        act(A("xc"), IND(A("xa", 0, 256 * (t + 1)), A("xo16")), AF.Copy)
        own = A("ag", 256 + 128 * rank, 384 + 128 * rank)
        if last:
            swap_end(r)
            act(A("yxs"), A("xc"), AF.Copy)
            dma("y", T.yx[:], A("yxs"), "o_x")
            tt(A("ycs"), zs(11), prs(4), OP.add)
            dma("y", T.yc[:], A("ycs"), "o_c")
            act(A("yts", 0, 128), row0, AF.Copy)
            dma("y", T.yt[0:16:2, :], A("yts", 0, 128), "o_t0")
            ts(A("w100"), prs(5), 2.5, OP.is_ge, 100.0, OP.mult)
            cp(own, row0)
        else:
            M = A("pf", 0, 16) if not exch else A("pv0", 0, 16)
            for h in range(2):
                mm(M, A("pt", 2 - 2 * h, 130 - 2 * h), A("mb", h, 32, 2), h == 0, False)
            mm(M, A("idp"), prs(0), False, True)
            mm(G, A("idp"), zs(12), True, False)
            mm(G, A("idn"), prs(3), False, False)
            mm(G, A("idk"), prs(1), False, False)
            mm(G, A("idp"), prs(1), False, False)
            mm(G, A("idn"), prs(0), False, False)
            mm(D, A("idp"), zs(11), True, False)
            mm(D, A("idn"), prs(2), False, False)
            if exch:
                swap_end(r)
            elif reorder:
                folds("rb", "miss", OP.is_gt, 0, 10)
            else:
                pre_j()
            cp(A("m16"), M)
            tt(A("cst"), zs(11), prs(4), OP.add)
            tt(A("sm"), IND(A("id2"), A("m16")), A("stl"), OP.mult)
            to_list(G, "sm", 16, False)
            zrep("xc", 0, 4)
            if t == 1:
                lists_init()
            if exch:
                pre_j()
                act(A("df"), A("pf", 0, 128), AF.Copy)
                ts(A("w100"), prs(5), 2.5, OP.is_ge, 100.0, OP.mult)
                ts(A("e300"), prs(5), 1.5, OP.is_le, 301.0, OP.mult)
                cp(own, row0)
            elif reorder:
                folds("rb", "miss", OP.is_gt, 10, 16)
                swap()
            cp(A("gi"), G)
            ts(A("ga"), A("gi"), 8, OP.arith_shift_right)
            ts(A("gb"), A("gi"), 255, OP.bitwise_and)
            if not exch:
                cp(A("oh16", 0, 32), A("ga", 0, 32))
                act(A("oht"), IND(A("oh32"), A("oh16")), AF.Copy)
                if reorder:
                    swap_end(None)
            ts(A("f2i"), A("gi"), 4094, OP.bitwise_and)
            ts(A("fhi"), A("gi"), 254, OP.bitwise_and)
            if not exch:
                tt(A("om"), IND(A("ag", 0, 256), A("oo16")), A("oht"), OP.mult)
                to_list(D, "om", 16, False)
            zrep("xc", 4, 8)
            if not exch:
                if reorder:
                    act(A("df"), A("pf", 0, 128), AF.Copy)
                    pre_j()
                ts(A("w100"), prs(5), 2.5, OP.is_ge, 100.0, OP.mult)
                ts(A("e300"), prs(5), 1.5, OP.is_le, 301.0, OP.mult)
            cp(zs(12), A("f2i"))
            tt(A("fhk"), A("fhi"), A("e300"), OP.add)
        if not exch:
            tt(A("thv"), A("thi"), A("w100"), OP.add)
            new_d()
            continue
        ts(A("q2i"), A("gi"), 14, OP.bitwise_and)
        ts(A("hp"), A("gi"), 1, OP.arith_shift_right, 7, OP.bitwise_and)
        ts(A("fli"), A("gi"), 8, OP.arith_shift_right, 15, OP.bitwise_and)
        cp(A("q16", 0, 16), A("q2i"))
        tt(A("key"), A("hp"), A("w100"), OP.subtract)
        ts(A("q16", 16, 32), A("q2i"), 1.0, OP.add)
        ts(A("fl16"), A("fli"), 16.0, OP.add)
        act(A("ohf"), IND(A("oh32"), A("fl16")), AF.Copy)
        tt(A("wq"), IND(A("key"), A("bc16", 0, 8)), A("qc"), OP.is_equal)
        cp(A("fx16", 0, 16), A("fhi"))
        scan(A("wsc"), A("rs0", 0, 128), A("wq"), OP.mult, OP.add)
        mm(A("pc", 0, 128), A("tge"), A("wq"), True, False)
        mm(A("pc", 0, 128), A("bo"), A("wsc"), False, True)
        tt(A("uw", 0, 256), IND(A("hwt"), A("q16", 0, 16)), A("xc"), OP.mult)
        tt(A("tw", 0, 128), A("wq"), A("pc", 0, 128), OP.mult)
        tt(A("uw", 256, 512), IND(A("hwt"), A("q16", 16, 32)), A("xc"), OP.mult)
        to_list(A("pv0", 0, 32), "uw", 32, True)
        tt(A("tw", 128, 192), A("tw", 0, 64), A("tw", 64, 128), OP.add)
        ts(A("fx16", 16, 32), A("fhi"), 1.0, OP.add)
        tt(A("tw", 192, 224), A("tw", 128, 160), A("tw", 160, 192), OP.add)
        ts(A("q128"), A("q2i"), 64.0, OP.mult, 256.0, OP.add)
        tt(A("kk"), A("tw", 192, 208), A("tw", 208, 224), OP.add)
        act(A("wk0"), A("kk"), AF.Exp, scale=-math.log(4.0))
        tt(A("k2"), A("kk"), A("w100"), OP.subtract)
        cp(A("us"), A("pv0", 0, 16))
        ts(A("sv"), A("k2"), -84.5, OP.is_le)
        tt(A("hp"), A("us"), A("pv0", 16, 32), OP.mult)
        ts(A("sv_"), A("k2"), -84.5, OP.is_le)
        ts(A("hh"), A("hp"), 5, OP.arith_shift_right, 127, OP.bitwise_and)
        ts(A("hl"), A("hp"), 12, OP.arith_shift_right, 15, OP.bitwise_and)
        tt(A("wk"), A("wk0"), A("sv"), OP.mult)
        tt(A("ha", 0, 32), A("hl", 0, 32), A("c16", 0, 32), OP.add)
        if not last:
            ts(A("w2"), A("k2"), -84.5, OP.is_gt, 100.0, OP.mult)
            tt(A("ha", 0, 32), A("ha", 0, 32), A("ga", 0, 32), OP.subtract)
            tt(A("dk"), zs(11), A("sv"), OP.mult)
            tt(A("ha", 0, 32), A("ha", 0, 32), A("sv", 0, 32), OP.mult)
            tt(A("w2"), A("w2"), A("w100"), OP.min)
            tt(A("ha", 0, 32), A("ha", 0, 32), A("ga", 0, 32), OP.add)
            mm(D, A("idn"), A("dk"), False, False)
            tt(A("thv"), A("thi"), A("w2"), OP.add)
        cp(A("oh16", 0, 32), A("ha", 0, 32))
        act(A("oht"), IND(A("oh32"), A("oh16")), AF.Copy)
        tt(A("om2"), IND(A("ag", 0, 256), A("fx16", 16, 32)), A("ohf"), OP.mult)
        to_list(A("pg", 16, 32), "om2", 16, True)
        if t % 2 == 0 and not last:
            build_l()
        folds("rb", "wk", OP.mult, 0, 16)
        act(A("so", 0, 256, 2), A("pc", 0, 128), AF.Copy)
        if last:
            writers(0)
            writers(1)
        for grp, sem, cnt in ((from_direct, "ad%d" % r, n_direct), (from_relay, "ar%d" % r, n_relay)):
            arrive([x for q in grp for x in A("agu", r * 1024 + 128 * q, r * 1024 + 128 * q + 128)[1]], sem, cnt)
            for q in grp:
                cp(A("ag", 256 + 128 * q, 384 + 128 * q), A("agu", r * 1024 + 128 * q, r * 1024 + 128 * q + 128))
        tt(A("om"), IND(A("ag"), A("oo16")), A("oht"), OP.mult)
        to_list(D, "om", 16, last)
        if not last:
            writers(0)
            new_d()
        else:
            cp(zs(11), D)
            write_row1()
            ts(A("tw", 0, 128), A("pc", 0, 128), 2.0, OP.mult)
            tt(A("yts", 128, 256), A("tw", 0, 128), row1, OP.add)
            dma("y", T.yt[1:16:2, :], A("yts", 128, 256), "o_t1")

    known = {q: {} for q in Q}
    clocks = []
    waits = []
    need = set()
    for i, (q, call, deps, sem, cnt) in enumerate(ops):
        if q == "x":
            clocks.append({sem: 0})
            waits.append([])
            continue
        k = known[q]
        w = []
        for o in sorted(deps, reverse=True):
            tok = ops[o][0] if ops[o][3] is None else ops[o][3]
            lvl = o if ops[o][3] is None else 0
            if k.get(tok, -1) >= lvl:
                continue
            w.append(o)
            need.add(o)
            for a, b in clocks[o].items():
                if k.get(a, -1) < b:
                    k[a] = b
        waits.append(w)
        ck = dict(k)
        ck[q if sem is None else sem] = i if sem is None else 0
        clocks.append(ck)
    esem = {"v": T.sem.e_v, "s": T.sem.e_s, "t": T.sem.e_t, "g": T.sem.e_g}
    count = {q: 0 for q in esem}
    level = {}
    for i, (q, call, deps, sem, cnt) in enumerate(ops):
        if q == "x":
            continue
        for o in waits[i]:
            if ops[o][3] is None:
                Q[q].wait_ge(esem[ops[o][0]], level[o])
            else:
                Q[q].wait_ge(T.sem[ops[o][3]], ops[o][4])
        ins = call()
        if sem is None:
            if i in need:
                count[q] += 1
                level[i] = count[q]
                ins.then_inc(esem[q], 1)
        elif cnt > 0:
            ins.then_inc(T.sem[sem], cnt)
    g.wait_ge(T.sem.sent, nsent[0])
    for s in ("o_c", "o_x", "o_t0", "o_t1"):
        g.wait_ge(T.sem[s], 16)
